import numpy as np
import ml_dtypes


def mxq(x, axis, fmt="e4m3"):
    dtype, down = {"e4m3": (ml_dtypes.float8_e4m3fn, 7), "e5m2": (ml_dtypes.float8_e5m2, 14)}[fmt]
    v = np.moveaxis(np.asarray(x, np.float32).astype(ml_dtypes.bfloat16).astype(np.float64), axis, -1)
    blocks = v.reshape(v.shape[:-1] + (-1, 32))
    amax = np.abs(blocks).max(-1, keepdims=True)
    byte = np.maximum(np.where(amax > 0, np.frexp(amax)[1] - 1 + 127, 0) - down, 1)
    scale = np.exp2(byte - 127.0)
    codes = (blocks / scale).astype(np.float32).astype(dtype).astype(np.float64)
    return np.moveaxis((codes * scale).reshape(v.shape), -1, axis)


WIDE = False


def mx_kscale(k):
    if not WIDE:
        return np.ones(k)
    levels = np.array([10, -10, 5, -5, 0])
    if k % 512:
        return np.exp2(np.random.permutation(np.resize(levels, k // 32))).repeat(32)
    a = np.empty((k // 512, 16))
    for p in range(k // 512):
        a[p, :8] = np.random.permutation(np.resize(levels, 8))
        for g in range(8):
            far = levels[np.abs(levels - a[p, g]) >= 10]
            a[p, g + 8] = far[np.random.randint(len(far))]
    return np.exp2(a.ravel()).repeat(32)


def f64(x):
    return np.asarray(x).astype(np.float64)


def striped(idx):
    return np.tile(idx.reshape(-1, 16).T, (8, 1)).astype(np.uint16)


def unstriped(offs):
    return offs[:16].T.reshape(-1).astype(np.int64)


E2M1 = np.array([0.0, 0.5, 1.0, 1.5, 2.0, 3.0, 4.0, 6.0, -0.0, -0.5, -1.0, -1.5, -2.0, -3.0, -4.0, -6.0])


def pack_weight(w, fmt):
    k, n = w.shape
    w = f64(np.asarray(w, np.float32).astype(ml_dtypes.bfloat16)).reshape(k // 32, 32, n)
    amax = np.abs(w).max(1)
    if fmt == "e4m3":
        byte = np.frexp(amax)[1] - 1 + 127 - 7
    else:
        mant, ex = np.frexp(amax / 6.0)
        byte = np.where(mant > 0.5, ex, ex - 1) + 127
    byte = np.clip(np.where(amax > 0, byte, 1), 1, 254)
    scaled = (w * np.exp2(127.0 - byte)[:, None, :]).reshape(k, n).astype(np.float32)
    by_word = np.ascontiguousarray(scaled.reshape(k // 512, 128, 4, n).transpose(0, 1, 3, 2))
    if fmt == "e4m3":
        words = by_word.astype(ml_dtypes.float8_e4m3fn).view(np.uint8)
    else:
        c = by_word.astype(ml_dtypes.float4_e2m1fn).view(np.uint8) & 0xF
        words = (c[..., 0::2] | (c[..., 1::2] << 4)).reshape(k // 512, 128, 2 * n)
    return np.ascontiguousarray(words), np.ascontiguousarray(byte.astype(np.uint8).reshape(k // 512, 16, n))


def unpack_weight(words, scales, fmt):
    g, _, n = scales.shape
    words = np.ascontiguousarray(words).reshape(g, 128, n, -1)
    if fmt == "e4m3":
        vals = words.view(ml_dtypes.float8_e4m3fn).astype(np.float64)
    else:
        nib = np.empty((g, 128, n, 4), np.uint8)
        nib[..., 0::2] = words & 0xF
        nib[..., 1::2] = words >> 4
        vals = E2M1[nib]
    vals = vals * np.repeat(np.exp2(scales.astype(np.float64) - 127.0), 8, axis=1)[..., None]
    return vals.transpose(0, 1, 3, 2).reshape(g * 512, n)


def gelu(v):
    return 0.5 * v * (1.0 + np.tanh(np.sqrt(2.0 / np.pi) * (v + 0.044715 * v**3)))


def striped8(idx):
    return np.concatenate([v.reshape(-1, 16).T for v in idx]).astype(np.uint16)


def unstriped8(offs):
    return np.stack([offs[16 * g:16 * g + 16].T.reshape(-1) for g in range(8)]).astype(np.int64)


def heads(h, wgt, idx8):
    r = np.arange(h.shape[0])
    return wgt[r // 4 % 128] * h[r[:, None], idx8[r % 512 // 64]]


def put_heads(h, wgs, idx8, t2):
    r = np.arange(h.shape[0])
    page = np.zeros((h.shape[0], t2))
    page[r[:, None], idx8[r % 512 // 64]] = wgs[r // 4 % 128] * h
    return page


K, H, N, T, S, P, T2 = 512, 1024, 384, 4096, 1024, 1024, 2048

def setup_inputs():
    n = np.random.standard_normal
    s = mx_kscale(K)[:, None]
    u = mx_kscale(H)[:, None]
    d = {}
    d["tab_words"], d["tab_scales"] = pack_weight(n((K, T)) * s, "e4m3")
    d["offs"] = striped(np.random.permutation(T)[:S])
    d["offs2"] = striped8(np.stack([np.random.permutation(T2)[:S] for _ in range(8)]))
    d["offs3"] = striped8(np.stack([np.random.permutation(T2)[:P] for _ in range(8)]))
    d["w1"] = (1.3 * n((K, H)) / K**0.5 / s).astype(np.float32)
    d["w2_words"], d["w2_scales"] = pack_weight(0.8 * n((K, H)) / K**0.5 / s, "e4m3")
    d["wgs"] = np.repeat(np.random.uniform(0.5, 2.0, (8, S)), 16, axis=0).astype(np.float32)
    d["wgt"] = np.repeat(np.random.uniform(0.5, 2.0, (8, P)), 16, axis=0).astype(np.float32)
    d["root"] = (n((H, P)) * u).astype(np.float32)
    d["w3"] = (0.8 * n((H, N)) / H**0.5 / u).astype(np.float32)
    d["w4_words"], d["w4_scales"] = pack_weight(0.8 * n((H, N)) / H**0.5 / u, "e2m1")
    return d

def reference(tab_words, tab_scales, offs, offs2, offs3, w1, w2_words, w2_scales,
              wgs, wgt, root, w3, w4_words, w4_scales):
    v = unpack_weight(tab_words, tab_scales, "e4m3")[:, unstriped(offs)]
    bent = np.tanh(mxq(f64(w1), 0, "e4m3").T @ v)
    carried = unpack_weight(w2_words, w2_scales, "e4m3").T @ v
    h = bent + carried
    page = put_heads(h, f64(wgs), unstriped8(offs2), T2)
    x = heads(page, f64(wgt), unstriped8(offs3))
    rt = f64(root)
    z = mxq(x * rt + rt, 0, "e4m3")
    e1 = mxq(f64(w3), 0, "e4m3").T @ z
    e2 = unpack_weight(w4_words, w4_scales, "e2m1").T @ z
    return e2 * np.tanh(e1) + e1

@@ -1,0 +1,261 @@
+from contextlib import ExitStack
+
+import concourse.mybir as mybir
+from concourse.masks import make_identity
+
+K, H, N, T, S, M, T2 = 512, 1024, 384, 4096, 1024, 1024, 2048
+FLOPS = 2 * 2 * K * H * S + 2 * 2 * H * N * M
+
+F32 = mybir.dt.float32
+BF16 = mybir.dt.bfloat16
+I32 = mybir.dt.int32
+U32 = mybir.dt.uint32
+U16 = mybir.dt.uint16
+U8 = mybir.dt.uint8
+FP8X4 = mybir.dt.float8_e4m3fn_x4
+FP4X4 = mybir.dt.float4_e2m1fn_x4
+MULT = mybir.AluOpType.mult
+ADD = mybir.AluOpType.add
+TANH = mybir.ActivationFunctionType.Tanh
+
+P = 128
+PACK = 4
+PASS = P * PACK
+PASSES = H // PASS
+N_TILES = N // P
+PER_COLUMN = 16
+
+TABLE_CUTS = (256, 768)
+TABLE_LOADS = 4
+PUT_CUTS = ((128, 128, 128, 128, 256, 256), (512, 512))
+W1_AFTER_CUT = 3
+RING = 4
+FIRST_READ_CUTS = (512, 512)
+LAST_READ_CUTS = (256, 256, 256, 128, 128)
+STAGES = 3
+MX_BANKS = 6
+
+
+def spans(widths):
+    starts = [sum(widths[:n]) for n in range(len(widths))]
+    return list(zip(starts, widths))
+
+
+def entries(offsets, start, width):
+    return offsets[:, start // PER_COLUMN : (start + width) // PER_COLUMN]
+
+
+def weave(engine_copy, dst, src, width):
+    engine_copy(
+        out=dst.rearrange("p (c q i) -> p c i q", q=4, i=PACK),
+        in_=src.rearrange("p i (c q) -> p c i q", q=4),
+    )
+
+
+def tile_list_aligner_staging_features_kernel(
+    tc, tab_words, tab_scales, offs, offs2, offs3, w1, w2_words, w2_scales,
+    wgs, wgt, root, w3, w4_words, w4_scales, out,
+):
+    nc = tc.nc
+    with ExitStack() as ctx:
+        lists = ctx.enter_context(tc.tile_pool(name="lists", bufs=1))
+        keep = ctx.enter_context(tc.tile_pool(name="keep", bufs=1))
+        shared = ctx.enter_context(tc.tile_pool(name="shared", bufs=1))
+        psum = ctx.enter_context(tc.psum_pool(name="psum", bufs=1))
+
+        def sbuf(name, shape, dtype):
+            return keep.tile(shape, dtype, name=name, align_bytes=64)
+
+        pick = lists.tile([P, S // PER_COLUMN], U16, name="pick")
+        put = lists.tile([P, S // PER_COLUMN], U16, name="put")
+        read = lists.tile([P, M // PER_COLUMN], U16, name="read")
+
+        tab_w = shared.tile([P, T], I32, name="tab_w", offset=0)
+        tab_s = keep.tile([P, T], U8, name="tab_s", tag="scales_then_words", align_bytes=64)
+        raw = [sbuf("raw%d" % b, [P, PACK, PASS], F32) for b in range(PASSES)]
+        woven_w = [sbuf("woven_w%d" % b, [P, PACK * PASS], BF16) for b in range(PASSES)]
+        w1_w = [sbuf("w1_w%d" % b, [P, PASS], U32) for b in range(PASSES)]
+        w1_s = [sbuf("w1_s%d" % b, [P, PASS], U8) for b in range(PASSES)]
+        w2_w = [sbuf("w2_w%d" % b, [P, PASS], I32) for b in range(PASSES)]
+        w2_s = sbuf("w2_s", [P, H], U8)
+        w3_w = [sbuf("w3_w%d" % b, [P, N], U32) for b in range(PASSES)]
+        w3_s = [sbuf("w3_s%d" % b, [P, N], U8) for b in range(PASSES)]
+        w4_w = sbuf("w4_w", [P, PASSES, 2 * N], U8)
+        w4_s = sbuf("w4_s", [P, PASSES, N], U8)
+        wgs_t = sbuf("wgs_t", [P, S], F32)
+        wgt_t = sbuf("wgt_t", [P, M], F32)
+        root_t = [sbuf("root%d" % b, [P, PACK, M], F32) for b in range(PASSES)]
+        pages = [sbuf("page%d" % i, [P, T2], F32) for i in range(2)]
+        stage = [sbuf("stage%d" % n, [P, 2 * PASS], F32) for n in range(STAGES)]
+        h = [[sbuf("h%d_%d" % (b, n), [P, PACK, w], F32) for n, w in enumerate(PUT_CUTS[b])] for b in range(PASSES)]
+        x = [sbuf("x%d" % n, [P, PACK * 512], F32) for n in range(2)]
+        z_planes = [sbuf("z_planes%d" % n, [P, PACK * 512], BF16) for n in range(2)]
+        z_w = [sbuf("z_w%d" % b, [P, M], U32) for b in range(PASSES)]
+        z_s = [sbuf("z_s%d" % b, [P, M], U8) for b in range(PASSES)]
+        tanh_e1 = [sbuf("tanh_e1_%d" % n, [P, N], F32) for n in range(2)]
+        gated = [sbuf("gated%d" % n, [P, N], F32) for n in range(2)]
+        result = [sbuf("result%d" % n, [P, N_TILES, 256], F32) for n in range(2)]
+        ident = sbuf("ident", [P, P], F32)
+
+        mx_banks = [psum.tile([P, PASS], F32, name="mx_bank%d" % n) for n in range(MX_BANKS)]
+
+        def load_scale_rows(queue, dst, src):
+            for q in range(4):
+                queue.dma_start(out=dst(slice(32 * q, 32 * q + 4)).bitcast(I32), in_=src(slice(4 * q, 4 * q + 4)).bitcast(I32))
+
+        w1_rows = w1.rearrange("(p i) c -> p i c", i=PACK)
+        w2_bytes = w2_words[0].rearrange("p c i -> p (c i)")
+
+        nc.gpsimd.memset(w2_s[:].bitcast(I32), 0)
+        nc.vector.memset(tab_s[:].bitcast(I32), 0)
+        nc.sync.dma_start(pick[:], offs)
+        load_scale_rows(nc.sync, lambda rows: w2_s[rows, :], lambda rows: w2_scales[0, rows, :])
+        for half in range(2):
+            cols = slice(half * PASS // 2, (half + 1) * PASS // 2)
+            nc.sync.dma_start(out=raw[0][:, :, cols], in_=w1_rows[:, :, cols])
+        tab_rows = tab_words[0].rearrange("p t i -> p (t i)").bitcast(I32)
+        for start in range(0, T, T // TABLE_LOADS):
+            cols = slice(start, start + T // TABLE_LOADS)
+            nc.sync.dma_start(out=tab_w[:, cols], in_=tab_rows[:, cols])
+            if start == 0:
+                load_scale_rows(nc.sync, lambda rows: tab_s[rows, :], lambda rows: tab_scales[0, rows, :])
+        nc.sync.dma_start(out=w2_w[0][:], in_=w2_bytes[:, 0 : PACK * PASS].bitcast(I32))
+        nc.sync.dma_start(put[:], offs2)
+        nc.sync.dma_start(out=wgs_t[:], in_=wgs)
+        nc.sync.dma_start(read[:], offs3)
+        nc.sync.dma_start(out=raw[1][:], in_=w1_rows[:, :, PASS:])
+        nc.sync.dma_start(out=w2_w[1][:], in_=w2_bytes[:, PACK * PASS :].bitcast(I32))
+        nc.sync.dma_start(out=wgt_t[:], in_=wgt)
+        for b in range(PASSES):
+            nc.sync.dma_start(out=root_t[b][:], in_=root[b * PASS : (b + 1) * PASS, :].rearrange("(p i) m -> p i m", i=PACK))
+
+        make_identity(nc, ident[:])
+        for page in pages:
+            nc.vector.memset(page[:], 0.0)
+        nc.vector.memset(w4_s[:].rearrange("p b c -> p (b c)").bitcast(I32), 0)
+
+        def quantise(words, scales, woven):
+            nc.vector.quantize_mx(out=words.bitcast(FP8X4), scales=scales, in_=woven)
+
+        def make_w1(b, woven):
+            for half in range(2):
+                first = half * PASS // 2
+                weave(nc.scalar.copy, woven[:, PACK * first : PACK * (first + PASS // 2)], raw[b][:, :, first : first + PASS // 2], PASS // 2)
+            quantise(w1_w[b][:], w1_s[b][:], woven[:])
+
+        woven_first = keep.tile([P, PACK * PASS], BF16, name="woven_first", tag="woven_then_scales", align_bytes=64)
+        make_w1(0, woven_first)
+        v_s = keep.tile([P, S], U8, name="v_s", tag="woven_then_scales", align_bytes=64)
+        nc.vector.tensor_copy(v_s[:], tab_s[:].indirect(pick[:]))
+        v_w = keep.tile([P, S], U32, name="v_w", tag="scales_then_words", align_bytes=64)
+        for start, width in spans(TABLE_CUTS):
+            nc.vector.tensor_copy(v_w[:, start : start + width], tab_w[:].bitcast(U32).indirect(entries(pick, start, width)))
+        for n, engine in enumerate((nc.vector, nc.gpsimd)):
+            pages.append(shared.tile([P, T2], F32, name="page%d" % (2 + n), offset=n * T2 * 4))
+            engine.memset(pages[-1][:], 0.0)
+
+        def v_block(start):
+            return v_w[:, start : start + P].bitcast(FP8X4), v_s[:, start : start + P]
+
+        def make_h_block(b, cut, cut_start, start):
+            step = b * (S // P) + start // P
+            bent_bank, carried_bank, sum_bank = [mx_banks[(3 * step + role) % RING] for role in range(3)]
+            parts = woven_w[1][:].bitcast(F32) if step == W1_AFTER_CUT else stage[step % STAGES]
+            v_words, v_scales = v_block(start)
+            nc.tensor.matmul_mx(out=bent_bank[:], lhsT=v_words, lhsT_scale=v_scales,
+                                rhs=w1_w[b][:].bitcast(FP8X4), rhs_scale=w1_s[b][:], start=True, stop=True)
+            nc.tensor.matmul_mx(out=carried_bank[:], lhsT=v_words, lhsT_scale=v_scales,
+                                rhs=w2_w[b][:].bitcast(FP8X4), rhs_scale=w2_s[:, b * PASS : (b + 1) * PASS], start=True, stop=True)
+            nc.scalar.activation(out=parts[:, 0:PASS].rearrange("j (i p) -> j i p", i=PACK),
+                                 in_=bent_bank[:].rearrange("j (p i) -> j i p", i=PACK), func=TANH)
+            nc.scalar.copy(out=parts[:, PASS:].rearrange("j (i p) -> j i p", i=PACK),
+                           in_=carried_bank[:].rearrange("j (p i) -> j i p", i=PACK))
+            for i in range(PACK):
+                for term in range(2):
+                    first = term * PASS + i * P
+                    nc.tensor.matmul(sum_bank[:, i * P : (i + 1) * P], parts[:, first : first + P], ident[:],
+                                     is_transpose=True, start=(term == 0), stop=(term == 1))
+            nc.scalar.copy(out=h[b][cut][:, :, start - cut_start : start - cut_start + P],
+                           in_=sum_bank[:].rearrange("p (i j) -> p i j", i=PACK))
+
+        def put_h(b, cut, start, width):
+            for i in range(PACK):
+                nc.vector.tensor_tensor(pages[i][:].indirect(entries(put, start, width)), h[b][cut][:, i, :],
+                                        wgs_t[:, start : start + width], MULT)
+
+        def make_z(b, turn, start, width):
+            x_t = x[turn % 2][:, 0 : PACK * width].rearrange("p (i m) -> p i m", i=PACK)
+            planes = z_planes[turn % 2][:, 0 : PACK * width].rearrange("p (i m) -> p i m", i=PACK)
+            woven = stage[turn % STAGES][:].bitcast(BF16)[:, 0 : PACK * width]
+            for i in range(PACK):
+                nc.vector.tensor_tensor(x_t[:, i, :], pages[i][:].indirect(entries(read, start, width)),
+                                        wgt_t[:, start : start + width], MULT)
+            nc.vector.scalar_tensor_tensor(out=planes, in0=x_t, scalar=1.0, in1=root_t[b][:, :, start : start + width],
+                                           op0=ADD, op1=MULT)
+            return lambda: (
+                weave(nc.scalar.copy, woven, planes, width),
+                quantise(z_w[b][:, start : start + width], z_s[b][:, start : start + width], woven),
+            )
+
+        for cut, (cut_start, width) in enumerate(spans(PUT_CUTS[0])):
+            for start in range(cut_start, cut_start + width, P):
+                make_h_block(0, cut, cut_start, start)
+            put_h(0, cut, cut_start, width)
+            if cut == W1_AFTER_CUT:
+                make_w1(1, woven_w[1])
+        finish_first = [make_z(0, turn, start, width) for turn, (start, width) in enumerate(spans(FIRST_READ_CUTS))]
+
+        w3_raw = [raw[b][:].rearrange("p i c -> p (i c)")[:, 0 : PACK * N].rearrange("p (i c) -> p i c", i=PACK) for b in range(PASSES)]
+        for b in range(PASSES):
+            nc.sync.dma_start(out=w3_raw[b], in_=w3[b * PASS : (b + 1) * PASS, :].rearrange("(p i) c -> p i c", i=PACK))
+        nc.sync.dma_start(out=w4_w[:].bitcast(I32), in_=w4_words.rearrange("b p c -> p b c").bitcast(I32))
+        load_scale_rows(nc.sync, lambda rows: w4_s[rows, :, :], lambda rows: w4_scales[:, rows, :].rearrange("b q c -> q b c"))
+
+        for cut, (cut_start, width) in enumerate(spans(PUT_CUTS[1])):
+            for start in range(cut_start, cut_start + width, P):
+                make_h_block(1, cut, cut_start, start)
+            put_h(1, cut, cut_start, width)
+        for finish in finish_first:
+            finish()
+        for b in range(PASSES):
+            weave(nc.scalar.copy, woven_w[b][:, 0 : PACK * N], w3_raw[b], N)
+            quantise(w3_w[b][:], w3_s[b][:], woven_w[b][:, 0 : PACK * N])
+
+        def make_out(turn, cut_start, width):
+            staged = result[turn % 2]
+            for start in range(cut_start, cut_start + width, P):
+                step = start // P
+                e1 = mx_banks[(2 * step) % MX_BANKS]
+                e2 = mx_banks[(2 * step + 1) % MX_BANKS]
+                cols = slice(start, start + P)
+                for t in range(N_TILES):
+                    for b in range(PASSES):
+                        nc.tensor.matmul_mx(out=e1[:, t * P : (t + 1) * P],
+                                            lhsT=w3_w[b][:, t * P : (t + 1) * P].bitcast(FP8X4),
+                                            lhsT_scale=w3_s[b][:, t * P : (t + 1) * P],
+                                            rhs=z_w[b][:, cols].bitcast(FP8X4), rhs_scale=z_s[b][:, cols],
+                                            start=(b == 0), stop=(b == PASSES - 1))
+                for t in range(N_TILES):
+                    for b in range(PASSES):
+                        nc.tensor.matmul_mx(out=e2[:, t * P : (t + 1) * P],
+                                            lhsT=w4_w[:, b, 2 * t * P : 2 * (t + 1) * P].bitcast(FP4X4),
+                                            lhsT_scale=w4_s[:, b, t * P : (t + 1) * P],
+                                            rhs=z_w[b][:, cols].bitcast(FP8X4), rhs_scale=z_s[b][:, cols],
+                                            start=(b == 0), stop=(b == PASSES - 1))
+                nc.scalar.activation(out=tanh_e1[step % 2][:], in_=e1[:, 0:N], func=TANH)
+                nc.vector.tensor_tensor(gated[step % 2][:], e2[:, 0:N], tanh_e1[step % 2][:], MULT)
+                nc.vector.tensor_tensor(staged[:, :, start - cut_start : start - cut_start + P],
+                                        e1[:, 0:N].rearrange("n (t m) -> n t m", t=N_TILES),
+                                        gated[step % 2][:].rearrange("n (t m) -> n t m", t=N_TILES), ADD)
+            nc.sync.dma_start(out=out[:, cut_start : cut_start + width].rearrange("(t n) m -> n t m", t=N_TILES),
+                              in_=staged[:, :, 0:width])
+
+        cuts = spans(LAST_READ_CUTS)
+        first_turn = len(FIRST_READ_CUTS)
+        for turn in range(len(cuts) + 1):
+            if turn < len(cuts):
+                finish = make_z(1, first_turn + turn, *cuts[turn])
+            if turn > 0:
+                make_out(turn - 1, *cuts[turn - 1])
+            if turn < len(cuts):
+                finish()

@@ -27,13 +27,15 @@ PER_COLUMN = 16
 
 TABLE_CUTS = (256, 768)
 TABLE_LOADS = 4
-PUT_CUTS = ((128, 128, 128, 128, 256, 256), (512, 512))
+PUT_CUTS = ((128, 128, 128, 128, 256, 256), (1024,))
 W1_AFTER_CUT = 3
 RING = 4
-FIRST_READ_CUTS = (512, 512)
+FIRST_GROUPS = (1, 3)
+DIRECT_FROM = 512
+DEPTH = 2
 LAST_READ_CUTS = (256, 256, 256, 128, 128)
 STAGES = 3
-MX_BANKS = 6
+MX_BANKS = 8
 
 
 def spans(widths):
@@ -60,7 +62,6 @@ def tile_list_aligner_staging_features_kernel(
     with ExitStack() as ctx:
         lists = ctx.enter_context(tc.tile_pool(name="lists", bufs=1))
         keep = ctx.enter_context(tc.tile_pool(name="keep", bufs=1))
-        shared = ctx.enter_context(tc.tile_pool(name="shared", bufs=1))
         psum = ctx.enter_context(tc.psum_pool(name="psum", bufs=1))
 
         def sbuf(name, shape, dtype):
@@ -70,7 +71,7 @@ def tile_list_aligner_staging_features_kernel(
         put = lists.tile([P, S // PER_COLUMN], U16, name="put")
         read = lists.tile([P, M // PER_COLUMN], U16, name="read")
 
-        tab_w = shared.tile([P, T], I32, name="tab_w", offset=0)
+        tab_w = keep.tile([P, T], I32, name="tab_w", tag="table_then_page", align_bytes=64)
         tab_s = keep.tile([P, T], U8, name="tab_s", tag="scales_then_words", align_bytes=64)
         raw = [sbuf("raw%d" % b, [P, PACK, PASS], F32) for b in range(PASSES)]
         woven_w = [sbuf("woven_w%d" % b, [P, PACK * PASS], BF16) for b in range(PASSES)]
@@ -85,16 +86,18 @@ def tile_list_aligner_staging_features_kernel(
         wgs_t = sbuf("wgs_t", [P, S], F32)
         wgt_t = sbuf("wgt_t", [P, M], F32)
         root_t = [sbuf("root%d" % b, [P, PACK, M], F32) for b in range(PASSES)]
-        pages = [sbuf("page%d" % i, [P, T2], F32) for i in range(2)]
-        stage = [sbuf("stage%d" % n, [P, 2 * PASS], F32) for n in range(STAGES)]
+        pages = [sbuf("page%d" % i, [P, T2], F32) for i in range(PACK - 1)]
+        stage_tile = sbuf("stage", [P, STAGES * 2 * PASS], F32)
+        stage = [stage_tile[:, n * 2 * PASS : (n + 1) * 2 * PASS] for n in range(STAGES)]
         h = [[sbuf("h%d_%d" % (b, n), [P, PACK, w], F32) for n, w in enumerate(PUT_CUTS[b])] for b in range(PASSES)]
-        x = [sbuf("x%d" % n, [P, PACK * 512], F32) for n in range(2)]
-        z_planes = [sbuf("z_planes%d" % n, [P, PACK * 512], BF16) for n in range(2)]
+        x = sbuf("x", [P, PACK * M], F32)
+        z_planes = sbuf("z_planes", [P, PACK * M], BF16)
         z_w = [sbuf("z_w%d" % b, [P, M], U32) for b in range(PASSES)]
         z_s = [sbuf("z_s%d" % b, [P, M], U8) for b in range(PASSES)]
-        tanh_e1 = [sbuf("tanh_e1_%d" % n, [P, N], F32) for n in range(2)]
-        gated = [sbuf("gated%d" % n, [P, N], F32) for n in range(2)]
-        result = [sbuf("result%d" % n, [P, N_TILES, 256], F32) for n in range(2)]
+        tanh_e1 = [sbuf("tanh_e1_%d" % n, [P, N], F32) for n in range(DEPTH)]
+        e1_copy = [sbuf("e1_copy%d" % n, [P, N], F32) for n in range(DEPTH)]
+        gated = [sbuf("gated%d" % n, [P, N], F32) for n in range(DEPTH)]
+        result = root_t[0][:, 0:N_TILES, :]
         ident = sbuf("ident", [P, P], F32)
 
         mx_banks = [psum.tile([P, PASS], F32, name="mx_bank%d" % n) for n in range(MX_BANKS)]
@@ -150,9 +153,8 @@ def tile_list_aligner_staging_features_kernel(
         v_w = keep.tile([P, S], U32, name="v_w", tag="scales_then_words", align_bytes=64)
         for start, width in spans(TABLE_CUTS):
             nc.vector.tensor_copy(v_w[:, start : start + width], tab_w[:].bitcast(U32).indirect(entries(pick, start, width)))
-        for n, engine in enumerate((nc.vector, nc.gpsimd)):
-            pages.append(shared.tile([P, T2], F32, name="page%d" % (2 + n), offset=n * T2 * 4))
-            engine.memset(pages[-1][:], 0.0)
+        pages.append(keep.tile([P, T2], F32, name="page3", tag="table_then_page", align_bytes=64))
+        nc.gpsimd.memset(pages[-1][:], 0.0)
 
         def v_block(start):
             return v_w[:, start : start + P].bitcast(FP8X4), v_s[:, start : start + P]
@@ -170,32 +172,36 @@ def tile_list_aligner_staging_features_kernel(
                                  in_=bent_bank[:].rearrange("j (p i) -> j i p", i=PACK), func=TANH)
             nc.scalar.copy(out=parts[:, PASS:].rearrange("j (i p) -> j i p", i=PACK),
                            in_=carried_bank[:].rearrange("j (p i) -> j i p", i=PACK))
-            for i in range(PACK):
-                for term in range(2):
-                    first = term * PASS + i * P
-                    nc.tensor.matmul(sum_bank[:, i * P : (i + 1) * P], parts[:, first : first + P], ident[:],
-                                     is_transpose=True, start=(term == 0), stop=(term == 1))
-            nc.scalar.copy(out=h[b][cut][:, :, start - cut_start : start - cut_start + P],
-                           in_=sum_bank[:].rearrange("p (i j) -> p i j", i=PACK))
+            dst = h[b][cut][:, :, start - cut_start : start - cut_start + P]
+            groups = FIRST_GROUPS if step == 0 else (PACK,)
+            for n, (first_plane, planes) in enumerate(spans(groups)):
+                bank = sum_bank if n == 0 else mx_banks[RING + n - 1]
+                for i in range(planes):
+                    for term in range(2):
+                        first = term * PASS + (first_plane + i) * P
+                        nc.tensor.matmul(bank[:, i * P : (i + 1) * P], parts[:, first : first + P], ident[:],
+                                         is_transpose=True, start=(term == 0), stop=(term == 1))
+                nc.scalar.copy(out=dst[:, first_plane : first_plane + planes, :],
+                               in_=bank[:, 0 : planes * P].rearrange("p (i j) -> p i j", i=planes))
 
         def put_h(b, cut, start, width):
             for i in range(PACK):
                 nc.vector.tensor_tensor(pages[i][:].indirect(entries(put, start, width)), h[b][cut][:, i, :],
                                         wgs_t[:, start : start + width], MULT)
 
-        def make_z(b, turn, start, width):
-            x_t = x[turn % 2][:, 0 : PACK * width].rearrange("p (i m) -> p i m", i=PACK)
-            planes = z_planes[turn % 2][:, 0 : PACK * width].rearrange("p (i m) -> p i m", i=PACK)
-            woven = stage[turn % STAGES][:].bitcast(BF16)[:, 0 : PACK * width]
-            for i in range(PACK):
+        def read_pages(b, x_t, order, start, width):
+            planes = z_planes[:, 0 : PACK * width].rearrange("p (i m) -> p i m", i=PACK)
+            for i in order:
                 nc.vector.tensor_tensor(x_t[:, i, :], pages[i][:].indirect(entries(read, start, width)),
                                         wgt_t[:, start : start + width], MULT)
             nc.vector.scalar_tensor_tensor(out=planes, in0=x_t, scalar=1.0, in1=root_t[b][:, :, start : start + width],
                                            op0=ADD, op1=MULT)
-            return lambda: (
-                weave(nc.scalar.copy, woven, planes, width),
-                quantise(z_w[b][:, start : start + width], z_s[b][:, start : start + width], woven),
-            )
+            return planes
+
+        def make_z(b, planes, woven_tile, start, width):
+            woven = woven_tile[:].bitcast(BF16)[:, 0 : PACK * width]
+            weave(nc.scalar.copy, woven, planes, width)
+            quantise(z_w[b][:, start : start + width], z_s[b][:, start : start + width], woven)
 
         for cut, (cut_start, width) in enumerate(spans(PUT_CUTS[0])):
             for start in range(cut_start, cut_start + width, P):
@@ -203,7 +209,7 @@ def tile_list_aligner_staging_features_kernel(
             put_h(0, cut, cut_start, width)
             if cut == W1_AFTER_CUT:
                 make_w1(1, woven_w[1])
-        finish_first = [make_z(0, turn, start, width) for turn, (start, width) in enumerate(spans(FIRST_READ_CUTS))]
+        first_planes = read_pages(0, x[:].rearrange("p (i m) -> p i m", i=PACK), range(PACK), 0, M)
 
         w3_raw = [raw[b][:].rearrange("p i c -> p (i c)")[:, 0 : PACK * N].rearrange("p (i c) -> p i c", i=PACK) for b in range(PASSES)]
         for b in range(PASSES):
@@ -215,47 +221,59 @@ def tile_list_aligner_staging_features_kernel(
             for start in range(cut_start, cut_start + width, P):
                 make_h_block(1, cut, cut_start, start)
             put_h(1, cut, cut_start, width)
-        for finish in finish_first:
-            finish()
+        make_z(0, first_planes, stage_tile, 0, M)
         for b in range(PASSES):
             weave(nc.scalar.copy, woven_w[b][:, 0 : PACK * N], w3_raw[b], N)
             quantise(w3_w[b][:], w3_s[b][:], woven_w[b][:, 0 : PACK * N])
 
+        def w3_part(b, first, width):
+            return w3_w[b][:, first : first + width].bitcast(FP8X4), w3_s[b][:, first : first + width]
+
+        def w4_part(b, first, width):
+            return w4_w[:, b, 2 * first : 2 * (first + width)].bitcast(FP4X4), w4_s[:, b, first : first + width]
+
+        def z_part(b, first):
+            return z_w[b][:, first : first + P].bitcast(FP8X4), z_s[b][:, first : first + P]
+
+        def out_block(start, dst):
+            step = start // P
+            e1, e2, sum_bank = [mx_banks[(3 * step + role) % MX_BANKS] for role in range(3)]
+            tanh_t, gated_t, e1_t = tanh_e1[step % DEPTH], gated[step % DEPTH], e1_copy[step % DEPTH]
+            last = start >= DIRECT_FROM
+            for bank, weight in ((e1, w3_part), (e2, w4_part)):
+                passes = [(b, first, width) for b in range(PASSES) for first, width in spans((P, P, P) if last else (2 * P, P))]
+                for n, (b, first, width) in enumerate(passes):
+                    sides = (weight(b, first, width), z_part(b, start))
+                    (s_words, s_scales), (m_words, m_scales) = sides if last else sides[::-1]
+                    nc.tensor.matmul_mx(out=bank[:, first : first + width], lhsT=s_words, lhsT_scale=s_scales,
+                                        rhs=m_words, rhs_scale=m_scales, start=(n == 0), stop=(n == len(passes) - 1))
+            nc.scalar.activation(out=tanh_t[:], in_=e1[:, 0:N], func=TANH)
+            nc.vector.tensor_tensor(gated_t[:], e2[:, 0:N], tanh_t[:], MULT)
+            if last:
+                nc.vector.tensor_tensor(dst, e1[:, 0:N].rearrange("n (t m) -> n t m", t=N_TILES),
+                                        gated_t[:].rearrange("n (t m) -> n t m", t=N_TILES), ADD)
+                return
+            nc.scalar.copy(out=e1_t[:], in_=e1[:, 0:N])
+            for t in range(N_TILES):
+                for term, src in enumerate((e1_t, gated_t)):
+                    nc.tensor.matmul(sum_bank[:, t * P : (t + 1) * P], src[:, t * P : (t + 1) * P], ident[:],
+                                     is_transpose=True, start=(term == 0), stop=(term == 1))
+            nc.scalar.copy(out=dst, in_=sum_bank[:, 0:N].rearrange("n (t m) -> n t m", t=N_TILES))
+
         def make_out(turn, cut_start, width):
-            staged = result[turn % 2]
+            staged = result[:, :, cut_start : cut_start + width]
             for start in range(cut_start, cut_start + width, P):
-                step = start // P
-                e1 = mx_banks[(2 * step) % MX_BANKS]
-                e2 = mx_banks[(2 * step + 1) % MX_BANKS]
-                cols = slice(start, start + P)
-                for t in range(N_TILES):
-                    for b in range(PASSES):
-                        nc.tensor.matmul_mx(out=e1[:, t * P : (t + 1) * P],
-                                            lhsT=w3_w[b][:, t * P : (t + 1) * P].bitcast(FP8X4),
-                                            lhsT_scale=w3_s[b][:, t * P : (t + 1) * P],
-                                            rhs=z_w[b][:, cols].bitcast(FP8X4), rhs_scale=z_s[b][:, cols],
-                                            start=(b == 0), stop=(b == PASSES - 1))
-                for t in range(N_TILES):
-                    for b in range(PASSES):
-                        nc.tensor.matmul_mx(out=e2[:, t * P : (t + 1) * P],
-                                            lhsT=w4_w[:, b, 2 * t * P : 2 * (t + 1) * P].bitcast(FP4X4),
-                                            lhsT_scale=w4_s[:, b, t * P : (t + 1) * P],
-                                            rhs=z_w[b][:, cols].bitcast(FP8X4), rhs_scale=z_s[b][:, cols],
-                                            start=(b == 0), stop=(b == PASSES - 1))
-                nc.scalar.activation(out=tanh_e1[step % 2][:], in_=e1[:, 0:N], func=TANH)
-                nc.vector.tensor_tensor(gated[step % 2][:], e2[:, 0:N], tanh_e1[step % 2][:], MULT)
-                nc.vector.tensor_tensor(staged[:, :, start - cut_start : start - cut_start + P],
-                                        e1[:, 0:N].rearrange("n (t m) -> n t m", t=N_TILES),
-                                        gated[step % 2][:].rearrange("n (t m) -> n t m", t=N_TILES), ADD)
+                out_block(start, result[:, :, start : start + P])
             nc.sync.dma_start(out=out[:, cut_start : cut_start + width].rearrange("(t n) m -> n t m", t=N_TILES),
-                              in_=staged[:, :, 0:width])
+                              in_=staged)
 
         cuts = spans(LAST_READ_CUTS)
-        first_turn = len(FIRST_READ_CUTS)
-        for turn in range(len(cuts) + 1):
-            if turn < len(cuts):
-                finish = make_z(1, first_turn + turn, *cuts[turn])
+        slots = x[:, 0 : (PACK + 1) * max(LAST_READ_CUTS)].rearrange("p (s m) -> p s m", s=PACK + 1)
+        for turn, (start, width) in enumerate(cuts):
+            odd = turn % 2
+            order = [(i - odd) % PACK for i in range(PACK)]
+            planes = read_pages(1, slots[:, odd : odd + PACK, 0:width], order, start, width)
+            make_z(1, planes, stage[turn % STAGES], start, width)
             if turn > 0:
                 make_out(turn - 1, *cuts[turn - 1])
-            if turn < len(cuts):
-                finish()
+        make_out(len(cuts) - 1, *cuts[-1])

@@ -27,14 +27,14 @@ PER_COLUMN = 16
 
 TABLE_CUTS = (256, 768)
 TABLE_LOADS = 4
-PUT_CUTS = ((128, 128, 128, 128, 256, 256), (1024,))
+PUT_CUTS = ((128, 128, 128, 128, 128, 128, 256), (512, 512))
 W1_AFTER_CUT = 3
-RING = 4
+RING = 5
 FIRST_GROUPS = (1, 3)
 DIRECT_FROM = 512
 DEPTH = 2
-LAST_READ_CUTS = (256, 256, 256, 128, 128)
-STAGES = 3
+LAST_READ_CUTS = (128, 256, 256, 256, 128)
+STAGES = 4
 MX_BANKS = 8
 
 
@@ -74,7 +74,7 @@ def tile_list_aligner_staging_features_kernel(
         tab_w = keep.tile([P, T], I32, name="tab_w", tag="table_then_page", align_bytes=64)
         tab_s = keep.tile([P, T], U8, name="tab_s", tag="scales_then_words", align_bytes=64)
         raw = [sbuf("raw%d" % b, [P, PACK, PASS], F32) for b in range(PASSES)]
-        woven_w = [sbuf("woven_w%d" % b, [P, PACK * PASS], BF16) for b in range(PASSES)]
+        woven_second = sbuf("woven_second", [P, PACK * PASS], BF16)
         w1_w = [sbuf("w1_w%d" % b, [P, PASS], U32) for b in range(PASSES)]
         w1_s = [sbuf("w1_s%d" % b, [P, PASS], U8) for b in range(PASSES)]
         w2_w = [sbuf("w2_w%d" % b, [P, PASS], I32) for b in range(PASSES)]
@@ -85,19 +85,22 @@ def tile_list_aligner_staging_features_kernel(
         w4_s = sbuf("w4_s", [P, PASSES, N], U8)
         wgs_t = sbuf("wgs_t", [P, S], F32)
         wgt_t = sbuf("wgt_t", [P, M], F32)
-        root_t = [sbuf("root%d" % b, [P, PACK, M], F32) for b in range(PASSES)]
+        root_first = [sbuf("root0_0", [P, PACK, PASS], F32),
+                      keep.tile([P, PACK, PASS], F32, name="root0_1", tag="root_then_codes", align_bytes=64)]
+        root_last = sbuf("root1", [P, PACK, M], F32)
         pages = [sbuf("page%d" % i, [P, T2], F32) for i in range(PACK - 1)]
         stage_tile = sbuf("stage", [P, STAGES * 2 * PASS], F32)
         stage = [stage_tile[:, n * 2 * PASS : (n + 1) * 2 * PASS] for n in range(STAGES)]
-        h = [[sbuf("h%d_%d" % (b, n), [P, PACK, w], F32) for n, w in enumerate(PUT_CUTS[b])] for b in range(PASSES)]
-        x = sbuf("x", [P, PACK * M], F32)
-        z_planes = sbuf("z_planes", [P, PACK * M], BF16)
-        z_w = [sbuf("z_w%d" % b, [P, M], U32) for b in range(PASSES)]
+        h_tiles = [sbuf("h%d" % b, [P, PACK * S], F32) for b in range(PASSES)]
+        h = [[h_tiles[b][:, PACK * s : PACK * (s + w)].rearrange("p (i j) -> p i j", i=PACK) for s, w in spans(PUT_CUTS[b])]
+             for b in range(PASSES)]
+        x = sbuf("x", [P, PACK + 1, M], F32)
         z_s = [sbuf("z_s%d" % b, [P, M], U8) for b in range(PASSES)]
         tanh_e1 = [sbuf("tanh_e1_%d" % n, [P, N], F32) for n in range(DEPTH)]
         e1_copy = [sbuf("e1_copy%d" % n, [P, N], F32) for n in range(DEPTH)]
         gated = [sbuf("gated%d" % n, [P, N], F32) for n in range(DEPTH)]
-        result = root_t[0][:, 0:N_TILES, :]
+        result = h_tiles[0][:, 0 : N_TILES * M].rearrange("n (t m) -> n t m", t=N_TILES)
+        last_planes = sbuf("last_planes", [P, PACK * max(LAST_READ_CUTS)], BF16)
         ident = sbuf("ident", [P, P], F32)
 
         mx_banks = [psum.tile([P, PASS], F32, name="mx_bank%d" % n) for n in range(MX_BANKS)]
@@ -129,8 +132,10 @@ def tile_list_aligner_staging_features_kernel(
         nc.sync.dma_start(out=raw[1][:], in_=w1_rows[:, :, PASS:])
         nc.sync.dma_start(out=w2_w[1][:], in_=w2_bytes[:, PACK * PASS :].bitcast(I32))
         nc.sync.dma_start(out=wgt_t[:], in_=wgt)
-        for b in range(PASSES):
-            nc.sync.dma_start(out=root_t[b][:], in_=root[b * PASS : (b + 1) * PASS, :].rearrange("(p i) m -> p i m", i=PACK))
+        root_rows = [root[b * PASS : (b + 1) * PASS, :].rearrange("(p i) m -> p i m", i=PACK) for b in range(PASSES)]
+        for half in range(2):
+            nc.sync.dma_start(out=root_first[half][:], in_=root_rows[0][:, :, half * PASS : (half + 1) * PASS])
+        nc.sync.dma_start(out=root_last[:], in_=root_rows[1])
 
         make_identity(nc, ident[:])
         for page in pages:
@@ -162,7 +167,7 @@ def tile_list_aligner_staging_features_kernel(
         def make_h_block(b, cut, cut_start, start):
             step = b * (S // P) + start // P
             bent_bank, carried_bank, sum_bank = [mx_banks[(3 * step + role) % RING] for role in range(3)]
-            parts = woven_w[1][:].bitcast(F32) if step == W1_AFTER_CUT else stage[step % STAGES]
+            parts = woven_second[:].bitcast(F32) if step == W1_AFTER_CUT else stage[step % STAGES]
             v_words, v_scales = v_block(start)
             nc.tensor.matmul_mx(out=bent_bank[:], lhsT=v_words, lhsT_scale=v_scales,
                                 rhs=w1_w[b][:].bitcast(FP8X4), rhs_scale=w1_s[b][:], start=True, stop=True)
@@ -190,11 +195,11 @@ def tile_list_aligner_staging_features_kernel(
                                         wgs_t[:, start : start + width], MULT)
 
         def read_pages(b, x_t, order, start, width):
-            planes = z_planes[:, 0 : PACK * width].rearrange("p (i m) -> p i m", i=PACK)
+            planes = last_planes[:, 0 : PACK * width].rearrange("p (i m) -> p i m", i=PACK)
             for i in order:
                 nc.vector.tensor_tensor(x_t[:, i, :], pages[i][:].indirect(entries(read, start, width)),
                                         wgt_t[:, start : start + width], MULT)
-            nc.vector.scalar_tensor_tensor(out=planes, in0=x_t, scalar=1.0, in1=root_t[b][:, :, start : start + width],
+            nc.vector.scalar_tensor_tensor(out=planes, in0=x_t, scalar=1.0, in1=root_last[:, :, start : start + width],
                                            op0=ADD, op1=MULT)
             return planes
 
@@ -208,23 +213,45 @@ def tile_list_aligner_staging_features_kernel(
                 make_h_block(0, cut, cut_start, start)
             put_h(0, cut, cut_start, width)
             if cut == W1_AFTER_CUT:
-                make_w1(1, woven_w[1])
-        first_planes = read_pages(0, x[:].rearrange("p (i m) -> p i m", i=PACK), range(PACK), 0, M)
-
+                make_w1(1, woven_second)
         w3_raw = [raw[b][:].rearrange("p i c -> p (i c)")[:, 0 : PACK * N].rearrange("p (i c) -> p i c", i=PACK) for b in range(PASSES)]
         for b in range(PASSES):
             nc.sync.dma_start(out=w3_raw[b], in_=w3[b * PASS : (b + 1) * PASS, :].rearrange("(p i) c -> p i c", i=PACK))
+        for b in range(PASSES):
+            woven = x[:, PASSES - 1 - b, :].bitcast(BF16)[:, 0 : PACK * N]
+            weave(nc.scalar.copy, woven, w3_raw[b], N)
+            quantise(w3_w[b][:], w3_s[b][:], woven)
+        x_first = x[:, 0:PACK, :]
+        for i in range(PACK):
+            nc.vector.tensor_copy(x_first[:, i, :], pages[i][:].indirect(read[:]))
+
         nc.sync.dma_start(out=w4_w[:].bitcast(I32), in_=w4_words.rearrange("b p c -> p b c").bitcast(I32))
         load_scale_rows(nc.sync, lambda rows: w4_s[rows, :, :], lambda rows: w4_scales[:, rows, :].rearrange("b q c -> q b c"))
 
         for cut, (cut_start, width) in enumerate(spans(PUT_CUTS[1])):
             for start in range(cut_start, cut_start + width, P):
                 make_h_block(1, cut, cut_start, start)
-            put_h(1, cut, cut_start, width)
-        make_z(0, first_planes, stage_tile, 0, M)
-        for b in range(PASSES):
-            weave(nc.scalar.copy, woven_w[b][:, 0 : PACK * N], w3_raw[b], N)
-            quantise(w3_w[b][:], w3_s[b][:], woven_w[b][:, 0 : PACK * N])
+
+        def spread(weights, start, width):
+            return weights[:, start : start + width].unsqueeze(1).to_broadcast([P, PACK, width])
+
+        first_planes = x_first[:, :, PASS:].bitcast(BF16)
+        halves = spans(PUT_CUTS[1])
+        for cut, (start, width) in enumerate(halves):
+            other = halves[1 - cut][0]
+            weighted = h_tiles[0][:, PACK * other : PACK * (other + width)].rearrange("p (i j) -> p i j", i=PACK)
+            for i in range(PACK):
+                nc.gpsimd.tensor_tensor(weighted[:, i, :], h[1][cut][:, i, :], wgs_t[:, start : start + width], MULT)
+                nc.vector.tensor_copy(pages[i][:].indirect(entries(put, start, width)), weighted[:, i, :])
+        plus_one = [stage_tile[:, 2 * 2 * PASS :].rearrange("p (i m) -> p i m", i=PACK), x_first[:, :, 0:PASS]]
+        for half, (start, width) in enumerate(halves):
+            nc.gpsimd.tensor_tensor(h[1][half], x_first[:, :, start : start + width], spread(wgt_t, start, width), MULT)
+            nc.scalar.add(plus_one[half], h[1][half], 1.0)
+        for half, (start, width) in enumerate(halves):
+            nc.gpsimd.tensor_tensor(first_planes[:, :, start : start + width], plus_one[half], root_first[half][:], MULT)
+        z_w = [keep.tile([P, M], U32, name="z_w0", tag="root_then_codes", align_bytes=64), sbuf("z_w1", [P, M], U32)]
+        for half, (start, width) in enumerate(halves):
+            make_z(0, first_planes[:, :, start : start + width], stage[half], start, width)
 
         def w3_part(b, first, width):
             return w3_w[b][:, first : first + width].bitcast(FP8X4), w3_s[b][:, first : first + width]
@@ -268,11 +295,10 @@ def tile_list_aligner_staging_features_kernel(
                               in_=staged)
 
         cuts = spans(LAST_READ_CUTS)
-        slots = x[:, 0 : (PACK + 1) * max(LAST_READ_CUTS)].rearrange("p (s m) -> p s m", s=PACK + 1)
         for turn, (start, width) in enumerate(cuts):
             odd = turn % 2
             order = [(i - odd) % PACK for i in range(PACK)]
-            planes = read_pages(1, slots[:, odd : odd + PACK, 0:width], order, start, width)
+            planes = read_pages(1, x[:, odd : odd + PACK, 0:width], order, start, width)
             make_z(1, planes, stage[turn % STAGES], start, width)
             if turn > 0:
                 make_out(turn - 1, *cuts[turn - 1])

@@ -86,15 +86,18 @@ def tile_list_aligner_staging_features_kernel(
         wgs_t = sbuf("wgs_t", [P, S], F32)
         wgt_t = sbuf("wgt_t", [P, M], F32)
         root_first = [sbuf("root0_0", [P, PACK, PASS], F32),
-                      keep.tile([P, PACK, PASS], F32, name="root0_1", tag="root_then_codes", align_bytes=64)]
+                      keep.tile([P, PACK, PASS], F32, name="root0_1", tag="root_then_x", align_bytes=64)]
         root_last = sbuf("root1", [P, PACK, M], F32)
         pages = [sbuf("page%d" % i, [P, T2], F32) for i in range(PACK - 1)]
         stage_tile = sbuf("stage", [P, STAGES * 2 * PASS], F32)
         stage = [stage_tile[:, n * 2 * PASS : (n + 1) * 2 * PASS] for n in range(STAGES)]
-        h_tiles = [sbuf("h%d" % b, [P, PACK * S], F32) for b in range(PASSES)]
-        h = [[h_tiles[b][:, PACK * s : PACK * (s + w)].rearrange("p (i j) -> p i j", i=PACK) for s, w in spans(PUT_CUTS[b])]
+        h_tiles = [sbuf("h0", [P, N_TILES * M], F32), sbuf("h1", [P, PACK * PASS], F32)]
+        h = [[h_tiles[b][:, PACK * s : PACK * (s + w)].rearrange("p (i j) -> p i j", i=PACK) for s, w in spans(PUT_CUTS[b])[:-1]]
              for b in range(PASSES)]
-        x = sbuf("x", [P, PACK + 1, M], F32)
+        h_last = keep.tile([P, PACK, PUT_CUTS[0][-1]], F32, name="h0_last", tag="h_then_weighted", align_bytes=64)
+        h[0].append(h_last)
+        h_second = keep.tile([P, PACK, PUT_CUTS[1][-1]], F32, name="h1_last", tag="h_then_codes", align_bytes=64)
+        h[1].append(h_second[:])
         z_s = [sbuf("z_s%d" % b, [P, M], U8) for b in range(PASSES)]
         tanh_e1 = [sbuf("tanh_e1_%d" % n, [P, N], F32) for n in range(DEPTH)]
         e1_copy = [sbuf("e1_copy%d" % n, [P, N], F32) for n in range(DEPTH)]
@@ -132,6 +135,9 @@ def tile_list_aligner_staging_features_kernel(
         nc.sync.dma_start(out=raw[1][:], in_=w1_rows[:, :, PASS:])
         nc.sync.dma_start(out=w2_w[1][:], in_=w2_bytes[:, PACK * PASS :].bitcast(I32))
         nc.sync.dma_start(out=wgt_t[:], in_=wgt)
+        w3_raw = [sbuf("w3_raw%d" % b, [P, PACK, N], F32) for b in range(PASSES)]
+        for b in range(PASSES):
+            nc.sync.dma_start(out=w3_raw[b][:], in_=w3[b * PASS : (b + 1) * PASS, :].rearrange("(p i) c -> p i c", i=PACK))
         root_rows = [root[b * PASS : (b + 1) * PASS, :].rearrange("(p i) m -> p i m", i=PACK) for b in range(PASSES)]
         for half in range(2):
             nc.sync.dma_start(out=root_first[half][:], in_=root_rows[0][:, :, half * PASS : (half + 1) * PASS])
@@ -214,16 +220,16 @@ def tile_list_aligner_staging_features_kernel(
             put_h(0, cut, cut_start, width)
             if cut == W1_AFTER_CUT:
                 make_w1(1, woven_second)
-        w3_raw = [raw[b][:].rearrange("p i c -> p (i c)")[:, 0 : PACK * N].rearrange("p (i c) -> p i c", i=PACK) for b in range(PASSES)]
         for b in range(PASSES):
-            nc.sync.dma_start(out=w3_raw[b], in_=w3[b * PASS : (b + 1) * PASS, :].rearrange("(p i) c -> p i c", i=PACK))
-        for b in range(PASSES):
-            woven = x[:, PASSES - 1 - b, :].bitcast(BF16)[:, 0 : PACK * N]
-            weave(nc.scalar.copy, woven, w3_raw[b], N)
-            quantise(w3_w[b][:], w3_s[b][:], woven)
-        x_first = x[:, 0:PACK, :]
-        for i in range(PACK):
-            nc.vector.tensor_copy(x_first[:, i, :], pages[i][:].indirect(read[:]))
+            woven = keep.tile([P, PACK * N], BF16, name="woven_w3_%d" % b, tag="x_half%d" % (1 - b), align_bytes=64)
+            weave(nc.scalar.copy, woven[:], w3_raw[b][:], N)
+            quantise(w3_w[b][:], w3_s[b][:], woven[:])
+        halves = spans(PUT_CUTS[1])
+        x_first = []
+        for half, (start, width) in enumerate(halves):
+            x_first.append(keep.tile([P, PACK, width], F32, name="x_first%d" % half, tag="x_half%d" % half, align_bytes=64))
+            for i in range(PACK):
+                nc.vector.tensor_copy(x_first[half][:, i, :], pages[i][:].indirect(entries(read, start, width)))
 
         nc.sync.dma_start(out=w4_w[:].bitcast(I32), in_=w4_words.rearrange("b p c -> p b c").bitcast(I32))
         load_scale_rows(nc.sync, lambda rows: w4_s[rows, :, :], lambda rows: w4_scales[:, rows, :].rearrange("b q c -> q b c"))
@@ -235,21 +241,18 @@ def tile_list_aligner_staging_features_kernel(
         def spread(weights, start, width):
             return weights[:, start : start + width].unsqueeze(1).to_broadcast([P, PACK, width])
 
-        first_planes = x_first[:, :, PASS:].bitcast(BF16)
-        halves = spans(PUT_CUTS[1])
-        for cut, (start, width) in enumerate(halves):
-            other = halves[1 - cut][0]
-            weighted = h_tiles[0][:, PACK * other : PACK * (other + width)].rearrange("p (i j) -> p i j", i=PACK)
-            for i in range(PACK):
-                nc.gpsimd.tensor_tensor(weighted[:, i, :], h[1][cut][:, i, :], wgs_t[:, start : start + width], MULT)
-                nc.vector.tensor_copy(pages[i][:].indirect(entries(put, start, width)), weighted[:, i, :])
-        plus_one = [stage_tile[:, 2 * 2 * PASS :].rearrange("p (i m) -> p i m", i=PACK), x_first[:, :, 0:PASS]]
+        weighted = [keep.tile([P, PACK, PASS], F32, name="weighted0", tag="h_then_weighted", align_bytes=64), x_first[0]]
+        plus_one = [stage_tile[:, 2 * 2 * PASS :].rearrange("p (i m) -> p i m", i=PACK), h[1][1]]
         for half, (start, width) in enumerate(halves):
-            nc.gpsimd.tensor_tensor(h[1][half], x_first[:, :, start : start + width], spread(wgt_t, start, width), MULT)
+            nc.gpsimd.tensor_tensor(weighted[half][:], h[1][half], spread(wgs_t, start, width), MULT)
+            for i in range(PACK):
+                nc.vector.tensor_copy(pages[i][:].indirect(entries(put, start, width)), weighted[half][:, i, :])
+            nc.gpsimd.tensor_tensor(h[1][half], x_first[half][:], spread(wgt_t, start, width), MULT)
             nc.scalar.add(plus_one[half], h[1][half], 1.0)
+        first_planes = keep.tile([P, PACK, M], BF16, name="first_planes", tag="x_half1", align_bytes=64)
         for half, (start, width) in enumerate(halves):
             nc.gpsimd.tensor_tensor(first_planes[:, :, start : start + width], plus_one[half], root_first[half][:], MULT)
-        z_w = [keep.tile([P, M], U32, name="z_w0", tag="root_then_codes", align_bytes=64), sbuf("z_w1", [P, M], U32)]
+        z_w = [keep.tile([P, M], U32, name="z_w0", tag="h_then_codes", align_bytes=64), sbuf("z_w1", [P, M], U32)]
         for half, (start, width) in enumerate(halves):
             make_z(0, first_planes[:, :, start : start + width], stage[half], start, width)
 
@@ -295,6 +298,7 @@ def tile_list_aligner_staging_features_kernel(
                               in_=staged)
 
         cuts = spans(LAST_READ_CUTS)
+        x = keep.tile([P, PACK + 1, max(LAST_READ_CUTS)], F32, name="x", tag="root_then_x", align_bytes=64)
         for turn, (start, width) in enumerate(cuts):
             odd = turn % 2
             order = [(i - odd) % PACK for i in range(PACK)]

from contextlib import ExitStack

import concourse.mybir as mybir
from concourse.masks import make_identity

K, H, N, T, S, M, T2 = 512, 1024, 384, 4096, 1024, 1024, 2048
FLOPS = 2 * 2 * K * H * S + 2 * 2 * H * N * M

F32 = mybir.dt.float32
BF16 = mybir.dt.bfloat16
I32 = mybir.dt.int32
U32 = mybir.dt.uint32
U16 = mybir.dt.uint16
U8 = mybir.dt.uint8
FP8X4 = mybir.dt.float8_e4m3fn_x4
FP4X4 = mybir.dt.float4_e2m1fn_x4
MULT = mybir.AluOpType.mult
ADD = mybir.AluOpType.add
TANH = mybir.ActivationFunctionType.Tanh

P = 128
PACK = 4
PASS = P * PACK
PASSES = H // PASS
N_TILES = N // P
PER_COLUMN = 16

TABLE_CUTS = (256, 768)
TABLE_LOADS = 4
PUT_CUTS = ((128, 128, 128, 128, 128, 128, 256), (512, 512))
W1_AFTER_CUT = 3
RING = 5
FIRST_GROUPS = (1, 3)
DIRECT_FROM = 512
DEPTH = 2
LAST_READ_CUTS = (128, 256, 256, 256, 128)
STAGES = 4
MX_BANKS = 8


def spans(widths):
    starts = [sum(widths[:n]) for n in range(len(widths))]
    return list(zip(starts, widths))


def entries(offsets, start, width):
    return offsets[:, start // PER_COLUMN : (start + width) // PER_COLUMN]


def weave(engine_copy, dst, src, width):
    engine_copy(
        out=dst.rearrange("p (c q i) -> p c i q", q=4, i=PACK),
        in_=src.rearrange("p i (c q) -> p c i q", q=4),
    )


def tile_list_aligner_staging_features_kernel(
    tc, tab_words, tab_scales, offs, offs2, offs3, w1, w2_words, w2_scales,
    wgs, wgt, root, w3, w4_words, w4_scales, out,
):
    nc = tc.nc
    with ExitStack() as ctx:
        lists = ctx.enter_context(tc.tile_pool(name="lists", bufs=1))
        keep = ctx.enter_context(tc.tile_pool(name="keep", bufs=1))
        psum = ctx.enter_context(tc.psum_pool(name="psum", bufs=1))

        def sbuf(name, shape, dtype):
            return keep.tile(shape, dtype, name=name, align_bytes=64)

        pick = lists.tile([P, S // PER_COLUMN], U16, name="pick")
        put = lists.tile([P, S // PER_COLUMN], U16, name="put")
        read = lists.tile([P, M // PER_COLUMN], U16, name="read")

        tab_w = keep.tile([P, T], I32, name="tab_w", tag="table_then_page", align_bytes=64)
        tab_s = keep.tile([P, T], U8, name="tab_s", tag="scales_then_words", align_bytes=64)
        raw = [sbuf("raw%d" % b, [P, PACK, PASS], F32) for b in range(PASSES)]
        woven_second = sbuf("woven_second", [P, PACK * PASS], BF16)
        w1_w = [sbuf("w1_w%d" % b, [P, PASS], U32) for b in range(PASSES)]
        w1_s = [sbuf("w1_s%d" % b, [P, PASS], U8) for b in range(PASSES)]
        w2_w = [sbuf("w2_w%d" % b, [P, PASS], I32) for b in range(PASSES)]
        w2_s = sbuf("w2_s", [P, H], U8)
        w3_w = [sbuf("w3_w%d" % b, [P, N], U32) for b in range(PASSES)]
        w3_s = [sbuf("w3_s%d" % b, [P, N], U8) for b in range(PASSES)]
        w4_w = sbuf("w4_w", [P, PASSES, 2 * N], U8)
        w4_s = sbuf("w4_s", [P, PASSES, N], U8)
        wgs_t = sbuf("wgs_t", [P, S], F32)
        wgt_t = sbuf("wgt_t", [P, M], F32)
        root_first = [sbuf("root0_0", [P, PACK, PASS], F32),
                      keep.tile([P, PACK, PASS], F32, name="root0_1", tag="root_then_x", align_bytes=64)]
        root_last = sbuf("root1", [P, PACK, M], F32)
        pages = [sbuf("page%d" % i, [P, T2], F32) for i in range(PACK - 1)]
        stage_tile = sbuf("stage", [P, STAGES * 2 * PASS], F32)
        stage = [stage_tile[:, n * 2 * PASS : (n + 1) * 2 * PASS] for n in range(STAGES)]
        h_tiles = [sbuf("h0", [P, N_TILES * M], F32), sbuf("h1", [P, PACK * PASS], F32)]
        h = [[h_tiles[b][:, PACK * s : PACK * (s + w)].rearrange("p (i j) -> p i j", i=PACK) for s, w in spans(PUT_CUTS[b])[:-1]]
             for b in range(PASSES)]
        h_last = keep.tile([P, PACK, PUT_CUTS[0][-1]], F32, name="h0_last", tag="h_then_weighted", align_bytes=64)
        h[0].append(h_last)
        h_second = keep.tile([P, PACK, PUT_CUTS[1][-1]], F32, name="h1_last", tag="h_then_codes", align_bytes=64)
        h[1].append(h_second[:])
        z_s = [sbuf("z_s%d" % b, [P, M], U8) for b in range(PASSES)]
        tanh_e1 = [sbuf("tanh_e1_%d" % n, [P, N], F32) for n in range(DEPTH)]
        e1_copy = [sbuf("e1_copy%d" % n, [P, N], F32) for n in range(DEPTH)]
        gated = [sbuf("gated%d" % n, [P, N], F32) for n in range(DEPTH)]
        result = h_tiles[0][:, 0 : N_TILES * M].rearrange("n (t m) -> n t m", t=N_TILES)
        last_planes = sbuf("last_planes", [P, PACK * max(LAST_READ_CUTS)], BF16)
        ident = sbuf("ident", [P, P], F32)

        mx_banks = [psum.tile([P, PASS], F32, name="mx_bank%d" % n) for n in range(MX_BANKS)]

        def load_scale_rows(queue, dst, src):
            for q in range(4):
                queue.dma_start(out=dst(slice(32 * q, 32 * q + 4)).bitcast(I32), in_=src(slice(4 * q, 4 * q + 4)).bitcast(I32))

        w1_rows = w1.rearrange("(p i) c -> p i c", i=PACK)
        w2_bytes = w2_words[0].rearrange("p c i -> p (c i)")

        nc.gpsimd.memset(w2_s[:].bitcast(I32), 0)
        nc.vector.memset(tab_s[:].bitcast(I32), 0)
        nc.sync.dma_start(pick[:], offs)
        load_scale_rows(nc.sync, lambda rows: w2_s[rows, :], lambda rows: w2_scales[0, rows, :])
        for half in range(2):
            cols = slice(half * PASS // 2, (half + 1) * PASS // 2)
            nc.sync.dma_start(out=raw[0][:, :, cols], in_=w1_rows[:, :, cols])
        tab_rows = tab_words[0].rearrange("p t i -> p (t i)").bitcast(I32)
        for start in range(0, T, T // TABLE_LOADS):
            cols = slice(start, start + T // TABLE_LOADS)
            nc.sync.dma_start(out=tab_w[:, cols], in_=tab_rows[:, cols])
            if start == 0:
                load_scale_rows(nc.sync, lambda rows: tab_s[rows, :], lambda rows: tab_scales[0, rows, :])
        nc.sync.dma_start(out=w2_w[0][:], in_=w2_bytes[:, 0 : PACK * PASS].bitcast(I32))
        nc.sync.dma_start(put[:], offs2)
        nc.sync.dma_start(out=wgs_t[:], in_=wgs)
        nc.sync.dma_start(read[:], offs3)
        nc.sync.dma_start(out=raw[1][:], in_=w1_rows[:, :, PASS:])
        nc.sync.dma_start(out=w2_w[1][:], in_=w2_bytes[:, PACK * PASS :].bitcast(I32))
        nc.sync.dma_start(out=wgt_t[:], in_=wgt)
        w3_raw = [sbuf("w3_raw%d" % b, [P, PACK, N], F32) for b in range(PASSES)]
        for b in range(PASSES):
            nc.sync.dma_start(out=w3_raw[b][:], in_=w3[b * PASS : (b + 1) * PASS, :].rearrange("(p i) c -> p i c", i=PACK))
        root_rows = [root[b * PASS : (b + 1) * PASS, :].rearrange("(p i) m -> p i m", i=PACK) for b in range(PASSES)]
        for half in range(2):
            nc.sync.dma_start(out=root_first[half][:], in_=root_rows[0][:, :, half * PASS : (half + 1) * PASS])
        nc.sync.dma_start(out=root_last[:], in_=root_rows[1])

        make_identity(nc, ident[:])
        for page in pages:
            nc.vector.memset(page[:], 0.0)
        nc.vector.memset(w4_s[:].rearrange("p b c -> p (b c)").bitcast(I32), 0)

        def quantise(words, scales, woven):
            nc.vector.quantize_mx(out=words.bitcast(FP8X4), scales=scales, in_=woven)

        def make_w1(b, woven):
            for half in range(2):
                first = half * PASS // 2
                weave(nc.scalar.copy, woven[:, PACK * first : PACK * (first + PASS // 2)], raw[b][:, :, first : first + PASS // 2], PASS // 2)
            quantise(w1_w[b][:], w1_s[b][:], woven[:])

        woven_first = keep.tile([P, PACK * PASS], BF16, name="woven_first", tag="woven_then_scales", align_bytes=64)
        make_w1(0, woven_first)
        v_s = keep.tile([P, S], U8, name="v_s", tag="woven_then_scales", align_bytes=64)
        nc.vector.tensor_copy(v_s[:], tab_s[:].indirect(pick[:]))
        v_w = keep.tile([P, S], U32, name="v_w", tag="scales_then_words", align_bytes=64)
        for start, width in spans(TABLE_CUTS):
            nc.vector.tensor_copy(v_w[:, start : start + width], tab_w[:].bitcast(U32).indirect(entries(pick, start, width)))
        pages.append(keep.tile([P, T2], F32, name="page3", tag="table_then_page", align_bytes=64))
        nc.gpsimd.memset(pages[-1][:], 0.0)

        def v_block(start):
            return v_w[:, start : start + P].bitcast(FP8X4), v_s[:, start : start + P]

        def make_h_block(b, cut, cut_start, start):
            step = b * (S // P) + start // P
            bent_bank, carried_bank, sum_bank = [mx_banks[(3 * step + role) % RING] for role in range(3)]
            parts = woven_second[:].bitcast(F32) if step == W1_AFTER_CUT else stage[step % STAGES]
            v_words, v_scales = v_block(start)
            nc.tensor.matmul_mx(out=bent_bank[:], lhsT=v_words, lhsT_scale=v_scales,
                                rhs=w1_w[b][:].bitcast(FP8X4), rhs_scale=w1_s[b][:], start=True, stop=True)
            nc.tensor.matmul_mx(out=carried_bank[:], lhsT=v_words, lhsT_scale=v_scales,
                                rhs=w2_w[b][:].bitcast(FP8X4), rhs_scale=w2_s[:, b * PASS : (b + 1) * PASS], start=True, stop=True)
            nc.scalar.activation(out=parts[:, 0:PASS].rearrange("j (i p) -> j i p", i=PACK),
                                 in_=bent_bank[:].rearrange("j (p i) -> j i p", i=PACK), func=TANH)
            nc.scalar.copy(out=parts[:, PASS:].rearrange("j (i p) -> j i p", i=PACK),
                           in_=carried_bank[:].rearrange("j (p i) -> j i p", i=PACK))
            dst = h[b][cut][:, :, start - cut_start : start - cut_start + P]
            groups = FIRST_GROUPS if step == 0 else (PACK,)
            for n, (first_plane, planes) in enumerate(spans(groups)):
                bank = sum_bank if n == 0 else mx_banks[RING + n - 1]
                for i in range(planes):
                    for term in range(2):
                        first = term * PASS + (first_plane + i) * P
                        nc.tensor.matmul(bank[:, i * P : (i + 1) * P], parts[:, first : first + P], ident[:],
                                         is_transpose=True, start=(term == 0), stop=(term == 1))
                nc.scalar.copy(out=dst[:, first_plane : first_plane + planes, :],
                               in_=bank[:, 0 : planes * P].rearrange("p (i j) -> p i j", i=planes))

        def put_h(b, cut, start, width):
            for i in range(PACK):
                nc.vector.tensor_tensor(pages[i][:].indirect(entries(put, start, width)), h[b][cut][:, i, :],
                                        wgs_t[:, start : start + width], MULT)

        def read_pages(b, x_t, order, start, width):
            planes = last_planes[:, 0 : PACK * width].rearrange("p (i m) -> p i m", i=PACK)
            for i in order:
                nc.vector.tensor_tensor(x_t[:, i, :], pages[i][:].indirect(entries(read, start, width)),
                                        wgt_t[:, start : start + width], MULT)
            nc.vector.scalar_tensor_tensor(out=planes, in0=x_t, scalar=1.0, in1=root_last[:, :, start : start + width],
                                           op0=ADD, op1=MULT)
            return planes

        def make_z(b, planes, woven_tile, start, width):
            woven = woven_tile[:].bitcast(BF16)[:, 0 : PACK * width]
            weave(nc.scalar.copy, woven, planes, width)
            quantise(z_w[b][:, start : start + width], z_s[b][:, start : start + width], woven)

        for cut, (cut_start, width) in enumerate(spans(PUT_CUTS[0])):
            for start in range(cut_start, cut_start + width, P):
                make_h_block(0, cut, cut_start, start)
            put_h(0, cut, cut_start, width)
            if cut == W1_AFTER_CUT:
                make_w1(1, woven_second)
        for b in range(PASSES):
            woven = keep.tile([P, PACK * N], BF16, name="woven_w3_%d" % b, tag="x_half%d" % (1 - b), align_bytes=64)
            weave(nc.scalar.copy, woven[:], w3_raw[b][:], N)
            quantise(w3_w[b][:], w3_s[b][:], woven[:])
        halves = spans(PUT_CUTS[1])
        x_first = []
        for half, (start, width) in enumerate(halves):
            x_first.append(keep.tile([P, PACK, width], F32, name="x_first%d" % half, tag="x_half%d" % half, align_bytes=64))
            for i in range(PACK):
                nc.vector.tensor_copy(x_first[half][:, i, :], pages[i][:].indirect(entries(read, start, width)))

        nc.sync.dma_start(out=w4_w[:].bitcast(I32), in_=w4_words.rearrange("b p c -> p b c").bitcast(I32))
        load_scale_rows(nc.sync, lambda rows: w4_s[rows, :, :], lambda rows: w4_scales[:, rows, :].rearrange("b q c -> q b c"))

        for cut, (cut_start, width) in enumerate(spans(PUT_CUTS[1])):
            for start in range(cut_start, cut_start + width, P):
                make_h_block(1, cut, cut_start, start)

        def spread(weights, start, width):
            return weights[:, start : start + width].unsqueeze(1).to_broadcast([P, PACK, width])

        weighted = [keep.tile([P, PACK, PASS], F32, name="weighted0", tag="h_then_weighted", align_bytes=64), x_first[0]]
        plus_one = [stage_tile[:, 2 * 2 * PASS :].rearrange("p (i m) -> p i m", i=PACK), h[1][1]]
        for half, (start, width) in enumerate(halves):
            nc.gpsimd.tensor_tensor(weighted[half][:], h[1][half], spread(wgs_t, start, width), MULT)
            for i in range(PACK):
                nc.vector.tensor_copy(pages[i][:].indirect(entries(put, start, width)), weighted[half][:, i, :])
            nc.gpsimd.tensor_tensor(h[1][half], x_first[half][:], spread(wgt_t, start, width), MULT)
            nc.scalar.add(plus_one[half], h[1][half], 1.0)
        first_planes = keep.tile([P, PACK, M], BF16, name="first_planes", tag="x_half1", align_bytes=64)
        for half, (start, width) in enumerate(halves):
            nc.gpsimd.tensor_tensor(first_planes[:, :, start : start + width], plus_one[half], root_first[half][:], MULT)
        z_w = [keep.tile([P, M], U32, name="z_w0", tag="h_then_codes", align_bytes=64), sbuf("z_w1", [P, M], U32)]
        for half, (start, width) in enumerate(halves):
            make_z(0, first_planes[:, :, start : start + width], stage[half], start, width)

        def w3_part(b, first, width):
            return w3_w[b][:, first : first + width].bitcast(FP8X4), w3_s[b][:, first : first + width]

        def w4_part(b, first, width):
            return w4_w[:, b, 2 * first : 2 * (first + width)].bitcast(FP4X4), w4_s[:, b, first : first + width]

        def z_part(b, first):
            return z_w[b][:, first : first + P].bitcast(FP8X4), z_s[b][:, first : first + P]

        def out_block(start, dst):
            step = start // P
            e1, e2, sum_bank = [mx_banks[(3 * step + role) % MX_BANKS] for role in range(3)]
            tanh_t, gated_t, e1_t = tanh_e1[step % DEPTH], gated[step % DEPTH], e1_copy[step % DEPTH]
            last = start >= DIRECT_FROM
            for bank, weight in ((e1, w3_part), (e2, w4_part)):
                passes = [(b, first, width) for b in range(PASSES) for first, width in spans((P, P, P) if last else (2 * P, P))]
                for n, (b, first, width) in enumerate(passes):
                    sides = (weight(b, first, width), z_part(b, start))
                    (s_words, s_scales), (m_words, m_scales) = sides if last else sides[::-1]
                    nc.tensor.matmul_mx(out=bank[:, first : first + width], lhsT=s_words, lhsT_scale=s_scales,
                                        rhs=m_words, rhs_scale=m_scales, start=(n == 0), stop=(n == len(passes) - 1))
            nc.scalar.activation(out=tanh_t[:], in_=e1[:, 0:N], func=TANH)
            nc.vector.tensor_tensor(gated_t[:], e2[:, 0:N], tanh_t[:], MULT)
            if last:
                nc.vector.tensor_tensor(dst, e1[:, 0:N].rearrange("n (t m) -> n t m", t=N_TILES),
                                        gated_t[:].rearrange("n (t m) -> n t m", t=N_TILES), ADD)
                return
            nc.scalar.copy(out=e1_t[:], in_=e1[:, 0:N])
            for t in range(N_TILES):
                for term, src in enumerate((e1_t, gated_t)):
                    nc.tensor.matmul(sum_bank[:, t * P : (t + 1) * P], src[:, t * P : (t + 1) * P], ident[:],
                                     is_transpose=True, start=(term == 0), stop=(term == 1))
            nc.scalar.copy(out=dst, in_=sum_bank[:, 0:N].rearrange("n (t m) -> n t m", t=N_TILES))

        def make_out(turn, cut_start, width):
            staged = result[:, :, cut_start : cut_start + width]
            for start in range(cut_start, cut_start + width, P):
                out_block(start, result[:, :, start : start + P])
            nc.sync.dma_start(out=out[:, cut_start : cut_start + width].rearrange("(t n) m -> n t m", t=N_TILES),
                              in_=staged)

        cuts = spans(LAST_READ_CUTS)
        x = keep.tile([P, PACK + 1, max(LAST_READ_CUTS)], F32, name="x", tag="root_then_x", align_bytes=64)
        for turn, (start, width) in enumerate(cuts):
            odd = turn % 2
            order = [(i - odd) % PACK for i in range(PACK)]
            planes = read_pages(1, x[:, odd : odd + PACK, 0:width], order, start, width)
            make_z(1, planes, stage[turn % STAGES], start, width)
            if turn > 0:
                make_out(turn - 1, *cuts[turn - 1])
        make_out(len(cuts) - 1, *cuts[-1])
